import numpy as np
import ml_dtypes


def mxq(x, axis, fmt="e4m3"):
    dtype, down = {"e4m3": (ml_dtypes.float8_e4m3fn, 7), "e5m2": (ml_dtypes.float8_e5m2, 14)}[fmt]
    v = np.moveaxis(np.asarray(x, np.float32).astype(ml_dtypes.bfloat16).astype(np.float64), axis, -1)
    blocks = v.reshape(v.shape[:-1] + (-1, 32))
    amax = np.abs(blocks).max(-1, keepdims=True)
    byte = np.maximum(np.where(amax > 0, np.frexp(amax)[1] - 1 + 127, 0) - down, 1)
    scale = np.exp2(byte - 127.0)
    codes = (blocks / scale).astype(np.float32).astype(dtype).astype(np.float64)
    return np.moveaxis((codes * scale).reshape(v.shape), -1, axis)


WIDE = False


def mx_kscale(k):
    if not WIDE:
        return np.ones(k)
    levels = np.array([10, -10, 5, -5, 0])
    if k % 512:
        return np.exp2(np.random.permutation(np.resize(levels, k // 32))).repeat(32)
    a = np.empty((k // 512, 16))
    for p in range(k // 512):
        a[p, :8] = np.random.permutation(np.resize(levels, 8))
        for g in range(8):
            far = levels[np.abs(levels - a[p, g]) >= 10]
            a[p, g + 8] = far[np.random.randint(len(far))]
    return np.exp2(a.ravel()).repeat(32)


def f64(x):
    return np.asarray(x).astype(np.float64)


def striped(idx):
    return np.tile(idx.reshape(-1, 16).T, (8, 1)).astype(np.uint16)


def unstriped(offs):
    return offs[:16].T.reshape(-1).astype(np.int64)


def striped8(idx):
    return np.concatenate([x.reshape(-1, 16).T for x in idx]).astype(np.uint16)


def runs(offs, k):
    lists = np.stack([offs[16 * r : 16 * r + 16].T.reshape(-1) for r in range(8)]).astype(np.int64)
    return lists[np.arange(k) % 512 // 64]


def pack_weight(w):
    k, n = w.shape
    w = f64(np.asarray(w, np.float32).astype(ml_dtypes.bfloat16)).reshape(k // 32, 32, n)
    amax = np.abs(w).max(1)
    byte = np.clip(np.where(amax > 0, np.frexp(amax)[1] - 1 + 127 - 7, 1), 1, 254)
    scaled = (w * np.exp2(127.0 - byte)[:, None, :]).reshape(k, n).astype(np.float32)
    words = np.ascontiguousarray(scaled.reshape(k // 512, 128, 4, n).transpose(0, 1, 3, 2)).astype(ml_dtypes.float8_e4m3fn).view(np.uint8)
    return words, np.ascontiguousarray(byte.astype(np.uint8).reshape(k // 512, 16, n))


def unpack_weight(words, scales):
    g, p, n, _ = words.shape
    vals = np.ascontiguousarray(words).view(ml_dtypes.float8_e4m3fn).astype(np.float64) * np.repeat(np.exp2(scales.astype(np.float64) - 127.0), 8, axis=1)[..., None]
    return vals.transpose(0, 1, 3, 2).reshape(g * 512, n)


K, T, S, N, G, H, W = 512, 2048, 256, 512, 2048, 512, 128


def setup_inputs():
    n = np.random.standard_normal
    s = mx_kscale(K)[:, None]
    u = mx_kscale(K)
    packed_xT = pack_weight(n((K, T)) * s)
    packed_dT = pack_weight(n((K, G)) / s)
    perm = np.random.permutation(S)
    return {
        "x_words": packed_xT[0],
        "x_scales": packed_xT[1],
        "d_words": packed_dT[0],
        "d_scales": packed_dT[1],
        "gn": (np.random.uniform(0.5, 1.5, (H, 1)) * u[:, None]).astype(np.float32),
        "w1": (n((H, N)) / np.sqrt(H) / u[:, None]).astype(np.float32),
        "offs": striped8(np.random.randint(0, T, (8, S))),
        "k1": striped8(np.random.randint(0, G, (8, H))),
        "n1": striped(np.random.permutation(S)),
        "n2": striped(np.random.permutation(S)),
        "n3": striped(perm[:W]),
        "n4": striped(perm[W:]),
    }


def reference(x_words, x_scales, d_words, d_scales, gn, w1, offs, k1, n1, n2, n3, n4):
    d_k1 = unpack_weight(d_words, d_scales)[np.arange(K)[:, None], runs(k1, K)]
    xq = unpack_weight(x_words, x_scales)[np.arange(K)[:, None], runs(offs, K)]
    h = 0.0625 * (d_k1.T @ xq)
    z = f64(gn) * (h[:, unstriped(n1)] - h[:, unstriped(n2)])
    h2 = mxq(f64(w1), 0, "e4m3").T @ mxq(z, 0, "e4m3")
    pa = h2[:, unstriped(n3)]
    pb = h2[:, unstriped(n4)]
    rb = pa - pb
    ra = 0.75 * (pa + pb)
    ds = np.zeros((N, S))
    ds[:, unstriped(n3)] = ra
    out = ds.copy()
    out[:, unstriped(n4)] = rb
    return out

@@ -1,0 +1,178 @@
+from contextlib import ExitStack
+
+import concourse.mybir as mybir
+
+K, T, S, N, G, H, W = 512, 2048, 256, 512, 2048, 512, 128
+FLOPS = 2 * K * H * S + 2 * H * N * S
+
+F32 = mybir.dt.float32
+BF16 = mybir.dt.bfloat16
+I32 = mybir.dt.int32
+U32 = mybir.dt.uint32
+U16 = mybir.dt.uint16
+U8 = mybir.dt.uint8
+FP8X4 = mybir.dt.float8_e4m3fn_x4
+COPY = mybir.ActivationFunctionType.Copy
+ALU = mybir.AluOpType
+
+P = 128
+PACK = 4
+CH = 128
+
+
+def tile_picked_hpqgaphaar_none_p_kernel(tc, x_words, x_scales, d_words, d_scales, gn, w1, offs, k1, n1, n2, n3, n4, out):
+    nc = tc.nc
+    with ExitStack() as ctx:
+        lists = ctx.enter_context(tc.tile_pool(name="lists", bufs=1))
+        sb = ctx.enter_context(tc.tile_pool(name="sb", bufs=1))
+        psum = ctx.enter_context(tc.psum_pool(name="psum", bufs=1))
+
+        k1_t = lists.tile([P, H // 16], U16, name="k1_t")
+        offs_t = lists.tile([P, S // 16], U16, name="offs_t")
+        n1_t = lists.tile([P, S // 16], U16, name="n1_t")
+        n2_t = lists.tile([P, S // 16], U16, name="n2_t")
+        n3_t = lists.tile([P, W // 16], U16, name="n3_t")
+        n4_t = lists.tile([P, W // 16], U16, name="n4_t")
+
+        ds_win = sb.tile([P, G], U8, name="ds_win", align_bytes=64)
+        xs_win = sb.tile([P, T], U8, name="xs_win", align_bytes=64)
+        gn_t = sb.tile([P, PACK], F32, name="gn_t")
+        nc.sync.dma_start(k1_t[:], k1)
+        nc.sync.dma_start(ds_win[:].bitcast(I32), d_scales[0].bitcast(I32).unsqueeze(1).broadcast_to([16, 8, G // 4]))
+        nc.sync.dma_start(offs_t[:], offs)
+        nc.sync.dma_start(xs_win[:].bitcast(I32), x_scales[0].bitcast(I32).unsqueeze(1).broadcast_to([16, 8, T // 4]))
+        dw_win = sb.tile([P, G], I32, name="dw_win", tag="big_d", align_bytes=64)
+        xw_win = sb.tile([P, T], I32, name="xw_win", align_bytes=64)
+        nc.sync.dma_start(dw_win[:], d_words[0].rearrange("p n t -> p (n t)").bitcast(I32))
+        nc.sync.dma_start(n1_t[:], n1)
+        nc.sync.dma_start(n2_t[:], n2)
+        nc.sync.dma_start(xw_win[:], x_words[0].rearrange("p n t -> p (n t)").bitcast(I32))
+        nc.sync.dma_start(gn_t[:], gn.rearrange("(p t) o -> p (t o)", t=PACK))
+        nc.sync.dma_start(n3_t[:], n3)
+        nc.sync.dma_start(n4_t[:], n4)
+
+        gs = sb.tile([P, PACK], F32, name="gs", tag="picked1")
+        nc.scalar.activation(gs[:], gn_t[:], COPY, scale=0.0625)
+
+        sg = sb.tile([P, H + S], U8, name="sg", align_bytes=64)
+        plane = sb.tile([P, H + S], U8, name="plane", align_bytes=64)
+        dealt = sb.tile([P, H + S], U8, name="dealt", align_bytes=64)
+        nc.vector.memset(plane[:].bitcast(I32), 0)
+        nc.vector.tensor_copy(sg[:, :H], ds_win[:].indirect(k1_t[:]))
+        nc.vector.tensor_copy(
+            dealt[:, :H].rearrange("p (t m) -> p t m", t=PACK),
+            sg[:, :H].rearrange("p (m t) -> p t m", t=PACK),
+        )
+        nc.vector.tensor_copy(sg[:, H:], xs_win[:].indirect(offs_t[:]))
+        nc.vector.tensor_copy(dealt[:, H:].bitcast(I32), sg[:, H:].bitcast(I32))
+        for q in range(0, P, 32):
+            nc.scalar.dma_start(plane[q : q + 4, :].bitcast(I32), dealt[q : q + 32 : 8, :].bitcast(I32))
+
+        dg = sb.tile([P, H], U32, name="dg", align_bytes=64)
+        dq = sb.tile([P, H], U32, name="dq", align_bytes=64)
+        xq = sb.tile([P, S], U32, name="xq", align_bytes=64)
+        nc.vector.tensor_copy(dg[:], dw_win[:].bitcast(U32).indirect(k1_t[:]))
+        nc.vector.tensor_copy(
+            dq[:].bitcast(I32).rearrange("p (t m) -> p t m", t=PACK),
+            dg[:].bitcast(I32).rearrange("p (m t) -> p t m", t=PACK),
+        )
+        nc.vector.tensor_copy(xq[:], xw_win[:].bitcast(U32).indirect(offs_t[:]))
+
+        w_raw = sb.tile([P, PACK, N], F32, name="w_raw", tag="big_d", align_bytes=64)
+        for half in range(2):
+            cols = slice(half * (N // 2), (half + 1) * (N // 2))
+            nc.sync.dma_start(w_raw[:, :, cols], w1.rearrange("(p j) m -> p j m", j=PACK)[:, :, cols])
+
+        hw = []
+        for t in range(PACK):
+            bank = psum.tile([P, S], F32, name=f"hb{t}", tag=f"bank{t}")
+            nc.tensor.matmul_mx(
+                out=bank[:],
+                lhsT=dq[:, t * P : (t + 1) * P].bitcast(FP8X4),
+                lhsT_scale=plane[:, t * P : (t + 1) * P],
+                rhs=xq[:].bitcast(FP8X4),
+                rhs_scale=plane[:, H:],
+                start=True,
+                stop=True,
+            )
+            win = sb.tile([P, S], F32, name=f"hw{t}")
+            if t == 0:
+                nc.scalar.activation(win[:], bank[:], COPY, scale=gs[:, t : t + 1])
+            else:
+                nc.vector.tensor_scalar(win[:], bank[:], gs[:, t : t + 1], None, ALU.mult)
+            hw.append(win)
+
+        wq = [sb.tile([P, P], U32, name=f"wq{m}", align_bytes=64) for m in range(PACK)]
+        ws = [sb.tile([P, P], U8, name=f"ws{m}", align_bytes=64) for m in range(PACK)]
+
+        def quant_w(m):
+            wb = sb.tile([P, P * PACK], BF16, name=f"wb{m}", align_bytes=64)
+            nc.vector.tensor_copy(
+                wb[:].rearrange("p (c i j) -> p c j i", i=4, j=PACK),
+                w_raw[:, :, m * P : (m + 1) * P].rearrange("p j (c i) -> p c j i", i=4),
+            )
+            nc.vector.quantize_mx(out=wq[m][:].bitcast(FP8X4), scales=ws[m][:], in_=wb[:])
+
+        zq = sb.tile([P, S], U32, name="zq", align_bytes=64)
+        zs = sb.tile([P, S], U8, name="zs", align_bytes=64)
+        h2w = [sb.tile([P, S], F32, name=f"h2w{m}") for m in range(PACK)]
+
+        def second(m, lo, hi, tag):
+            bank = psum.tile([P, hi - lo], F32, name=f"h2b{m}_{lo}", tag=tag)
+            nc.tensor.matmul_mx(
+                out=bank[:],
+                lhsT=wq[m][:].bitcast(FP8X4),
+                lhsT_scale=ws[m][:],
+                rhs=zq[:, lo:hi].bitcast(FP8X4),
+                rhs_scale=zs[:, lo:hi],
+                start=True,
+                stop=True,
+            )
+            nc.vector.tensor_copy(h2w[m][:, lo:hi], bank[:])
+
+        quant_w(0)
+        for c in range(S // CH):
+            lo, hi = c * CH, (c + 1) * CH
+            picked = sb.tile([P, 2, PACK, CH], F32, name=f"picked{c}", tag=f"picked{c}")
+            g1, g2 = picked[:, 0], picked[:, 1]
+            for t in range(PACK):
+                nc.scalar.activation(g1[:, t, :], hw[t][:].indirect(n1_t[:, lo // 16 : hi // 16]), COPY)
+                nc.scalar.activation(g2[:, t, :], hw[t][:].indirect(n2_t[:, lo // 16 : hi // 16]), COPY)
+            zb = sb.tile([P, CH * PACK], BF16, name=f"zb{c}", align_bytes=64)
+            nc.vector.tensor_tensor(
+                zb[:].rearrange("p (c i t) -> p c t i", i=4, t=PACK),
+                g1.rearrange("p t (c i) -> p c t i", i=4),
+                g2.rearrange("p t (c i) -> p c t i", i=4),
+                ALU.subtract,
+            )
+            nc.vector.quantize_mx(out=zq[:, lo:hi].bitcast(FP8X4), scales=zs[:, lo:hi], in_=zb[:])
+            second(0, lo, hi, f"bank{4 + c}")
+            if c == 0:
+                quant_w(1)
+
+        def pair(m):
+            pa = sb.tile([P, W], F32, name=f"pa{m}")
+            pb = sb.tile([P, W], F32, name=f"pb{m}")
+            nc.scalar.activation(pa[:], h2w[m][:].indirect(n3_t[:]), COPY)
+            nc.scalar.activation(pb[:], h2w[m][:].indirect(n4_t[:]), COPY)
+            sm = sb.tile([P, W], F32, name=f"sm{m}")
+            df = sb.tile([P, W], F32, name=f"df{m}")
+            nc.vector.tensor_tensor(sm[:], pa[:], pb[:], ALU.add)
+            nc.vector.tensor_tensor(df[:], pa[:], pb[:], ALU.subtract)
+            return sm, df
+
+        def put(m, sm, df):
+            res = sb.tile([P, S], F32, name=f"res{m}")
+            nc.scalar.activation(res[:].indirect(n3_t[:]), sm[:], COPY, scale=0.75)
+            nc.scalar.activation(res[:].indirect(n4_t[:]), df[:], COPY)
+            nc.sync.dma_start(out[m * P : (m + 1) * P, :], res[:])
+
+        held = pair(0)
+        for m in range(1, PACK):
+            second(m, 0, S, f"bank{m}")
+            if m + 1 < PACK:
+                quant_w(m + 1)
+            nxt = pair(m)
+            put(m - 1, *held)
+            held = nxt
+        put(PACK - 1, *held)

@@ -17,7 +17,7 @@ ALU = mybir.AluOpType
 
 P = 128
 PACK = 4
-CH = 128
+CHUNKS = (((0, 128), (128, 192)), ((192, 256),))
 
 
 def tile_picked_hpqgaphaar_none_p_kernel(tc, x_words, x_scales, d_words, d_scales, gn, w1, offs, k1, n1, n2, n3, n4, out):
@@ -47,7 +47,7 @@ def tile_picked_hpqgaphaar_none_p_kernel(tc, x_words, x_scales, d_words, d_scale
         nc.sync.dma_start(n1_t[:], n1)
         nc.sync.dma_start(n2_t[:], n2)
         nc.sync.dma_start(xw_win[:], x_words[0].rearrange("p n t -> p (n t)").bitcast(I32))
-        nc.sync.dma_start(gn_t[:], gn.rearrange("(p t) o -> p (t o)", t=PACK))
+        nc.gpsimd.dma_start(gn_t[:], gn.rearrange("(p t) o -> p (t o)", t=PACK))
         nc.sync.dma_start(n3_t[:], n3)
         nc.sync.dma_start(n4_t[:], n4)
 
@@ -102,16 +102,17 @@ def tile_picked_hpqgaphaar_none_p_kernel(tc, x_words, x_scales, d_words, d_scale
                 nc.vector.tensor_scalar(win[:], bank[:], gs[:, t : t + 1], None, ALU.mult)
             hw.append(win)
 
-        wq = [sb.tile([P, P], U32, name=f"wq{m}", align_bytes=64) for m in range(PACK)]
-        ws = [sb.tile([P, P], U8, name=f"ws{m}", align_bytes=64) for m in range(PACK)]
-
-        def quant_w(m):
-            wb = sb.tile([P, P * PACK], BF16, name=f"wb{m}", align_bytes=64)
+        wq = sb.tile([P, N], U32, name="wq", align_bytes=64)
+        ws = sb.tile([P, N], U8, name="ws", align_bytes=64)
+        w_bf = sb.tile([P, N * PACK], BF16, name="w_bf", tag="rounded", align_bytes=64)
+        for half in range(2):
+            cols = slice(half * (N // 2), (half + 1) * (N // 2))
+            wb = w_bf[:, cols.start * PACK : cols.stop * PACK]
             nc.vector.tensor_copy(
-                wb[:].rearrange("p (c i j) -> p c j i", i=4, j=PACK),
-                w_raw[:, :, m * P : (m + 1) * P].rearrange("p j (c i) -> p c j i", i=4),
+                wb.rearrange("p (c i j) -> p c j i", i=4, j=PACK),
+                w_raw[:, :, cols].rearrange("p j (c i) -> p c j i", i=4),
             )
-            nc.vector.quantize_mx(out=wq[m][:].bitcast(FP8X4), scales=ws[m][:], in_=wb[:])
+            nc.vector.quantize_mx(out=wq[:, cols].bitcast(FP8X4), scales=ws[:, cols], in_=wb)
 
         zq = sb.tile([P, S], U32, name="zq", align_bytes=64)
         zs = sb.tile([P, S], U8, name="zs", align_bytes=64)
@@ -121,34 +122,35 @@ def tile_picked_hpqgaphaar_none_p_kernel(tc, x_words, x_scales, d_words, d_scale
             bank = psum.tile([P, hi - lo], F32, name=f"h2b{m}_{lo}", tag=tag)
             nc.tensor.matmul_mx(
                 out=bank[:],
-                lhsT=wq[m][:].bitcast(FP8X4),
-                lhsT_scale=ws[m][:],
+                lhsT=wq[:, m * P : (m + 1) * P].bitcast(FP8X4),
+                lhsT_scale=ws[:, m * P : (m + 1) * P],
                 rhs=zq[:, lo:hi].bitcast(FP8X4),
                 rhs_scale=zs[:, lo:hi],
                 start=True,
                 stop=True,
             )
-            nc.vector.tensor_copy(h2w[m][:, lo:hi], bank[:])
+            return bank
 
-        quant_w(0)
-        for c in range(S // CH):
-            lo, hi = c * CH, (c + 1) * CH
-            picked = sb.tile([P, 2, PACK, CH], F32, name=f"picked{c}", tag=f"picked{c}")
+        first_banks = []
+        for c, pieces in enumerate(CHUNKS):
+            lo, hi = pieces[0][0], pieces[-1][1]
+            picked = sb.tile([P, 2, PACK, hi - lo], F32, name=f"picked{c}", tag=f"picked{c}")
             g1, g2 = picked[:, 0], picked[:, 1]
             for t in range(PACK):
                 nc.scalar.activation(g1[:, t, :], hw[t][:].indirect(n1_t[:, lo // 16 : hi // 16]), COPY)
                 nc.scalar.activation(g2[:, t, :], hw[t][:].indirect(n2_t[:, lo // 16 : hi // 16]), COPY)
-            zb = sb.tile([P, CH * PACK], BF16, name=f"zb{c}", align_bytes=64)
+            zb = sb.tile([P, (hi - lo) * PACK], BF16, name=f"zb{c}", tag="rounded", align_bytes=64)
             nc.vector.tensor_tensor(
                 zb[:].rearrange("p (c i t) -> p c t i", i=4, t=PACK),
                 g1.rearrange("p t (c i) -> p c t i", i=4),
                 g2.rearrange("p t (c i) -> p c t i", i=4),
                 ALU.subtract,
             )
-            nc.vector.quantize_mx(out=zq[:, lo:hi].bitcast(FP8X4), scales=zs[:, lo:hi], in_=zb[:])
-            second(0, lo, hi, f"bank{4 + c}")
-            if c == 0:
-                quant_w(1)
+            for a, b in pieces:
+                nc.vector.quantize_mx(out=zq[:, a:b].bitcast(FP8X4), scales=zs[:, a:b], in_=zb[:, (a - lo) * PACK : (b - lo) * PACK])
+                first_banks.append((a, b, second(0, a, b, f"bank{4 + len(first_banks)}")))
+        for a, b, bank in first_banks:
+            nc.scalar.copy(h2w[0][:, a:b], bank[:])
 
         def pair(m):
             pa = sb.tile([P, W], F32, name=f"pa{m}")
@@ -169,9 +171,7 @@ def tile_picked_hpqgaphaar_none_p_kernel(tc, x_words, x_scales, d_words, d_scale
 
         held = pair(0)
         for m in range(1, PACK):
-            second(m, 0, S, f"bank{m}")
-            if m + 1 < PACK:
-                quant_w(m + 1)
+            nc.vector.tensor_copy(h2w[m][:], second(m, 0, S, f"bank{m}")[:])
             nxt = pair(m)
             put(m - 1, *held)
             held = nxt

@@ -37,15 +37,19 @@ def tile_picked_hpqgaphaar_none_p_kernel(tc, x_words, x_scales, d_words, d_scale
         ds_win = sb.tile([P, G], U8, name="ds_win", align_bytes=64)
         xs_win = sb.tile([P, T], U8, name="xs_win", align_bytes=64)
         gn_t = sb.tile([P, PACK], F32, name="gn_t")
+        nc.vector.memset(xs_win[:].bitcast(I32), 0)
+        nc.sync.dma_start(xs_win[0:P:8, :].bitcast(I32), x_scales[0].bitcast(I32))
         nc.sync.dma_start(k1_t[:], k1)
         nc.sync.dma_start(ds_win[:].bitcast(I32), d_scales[0].bitcast(I32).unsqueeze(1).broadcast_to([16, 8, G // 4]))
         nc.sync.dma_start(offs_t[:], offs)
-        nc.sync.dma_start(xs_win[:].bitcast(I32), x_scales[0].bitcast(I32).unsqueeze(1).broadcast_to([16, 8, T // 4]))
         dw_win = sb.tile([P, G], I32, name="dw_win", tag="big_d", align_bytes=64)
         xw_win = sb.tile([P, T], I32, name="xw_win", align_bytes=64)
-        nc.sync.dma_start(dw_win[:], d_words[0].rearrange("p n t -> p (n t)").bitcast(I32))
+        d_src = d_words[0].rearrange("p n t -> p (n t)").bitcast(I32)
+        for lo, hi in ((0, 1024), (1024, 1280), (1280, 1536)):
+            nc.sync.dma_start(dw_win[:, lo:hi], d_src[:, lo:hi])
         nc.sync.dma_start(n1_t[:], n1)
         nc.sync.dma_start(n2_t[:], n2)
+        nc.sync.dma_start(dw_win[:, 1536:], d_src[:, 1536:])
         nc.sync.dma_start(xw_win[:], x_words[0].rearrange("p n t -> p (n t)").bitcast(I32))
         nc.gpsimd.dma_start(gn_t[:], gn.rearrange("(p t) o -> p (t o)", t=PACK))
         nc.sync.dma_start(n3_t[:], n3)
@@ -54,7 +58,7 @@ def tile_picked_hpqgaphaar_none_p_kernel(tc, x_words, x_scales, d_words, d_scale
         gs = sb.tile([P, PACK], F32, name="gs", tag="picked1")
         nc.scalar.activation(gs[:], gn_t[:], COPY, scale=0.0625)
 
-        sg = sb.tile([P, H + S], U8, name="sg", align_bytes=64)
+        sg = sb.tile([P, H + S], U8, name="sg", tag="gathered", align_bytes=64)
         plane = sb.tile([P, H + S], U8, name="plane", align_bytes=64)
         dealt = sb.tile([P, H + S], U8, name="dealt", align_bytes=64)
         nc.vector.memset(plane[:].bitcast(I32), 0)
@@ -68,7 +72,7 @@ def tile_picked_hpqgaphaar_none_p_kernel(tc, x_words, x_scales, d_words, d_scale
         for q in range(0, P, 32):
             nc.scalar.dma_start(plane[q : q + 4, :].bitcast(I32), dealt[q : q + 32 : 8, :].bitcast(I32))
 
-        dg = sb.tile([P, H], U32, name="dg", align_bytes=64)
+        dg = sb.tile([P, H], U32, name="dg", tag="gathered", align_bytes=64)
         dq = sb.tile([P, H], U32, name="dq", align_bytes=64)
         xq = sb.tile([P, S], U32, name="xq", align_bytes=64)
         nc.vector.tensor_copy(dg[:], dw_win[:].bitcast(U32).indirect(k1_t[:]))
@@ -79,9 +83,7 @@ def tile_picked_hpqgaphaar_none_p_kernel(tc, x_words, x_scales, d_words, d_scale
         nc.vector.tensor_copy(xq[:], xw_win[:].bitcast(U32).indirect(offs_t[:]))
 
         w_raw = sb.tile([P, PACK, N], F32, name="w_raw", tag="big_d", align_bytes=64)
-        for half in range(2):
-            cols = slice(half * (N // 2), (half + 1) * (N // 2))
-            nc.sync.dma_start(w_raw[:, :, cols], w1.rearrange("(p j) m -> p j m", j=PACK)[:, :, cols])
+        nc.sync.dma_start(w_raw[:], w1.rearrange("(p j) m -> p j m", j=PACK))
 
         hw = []
         for t in range(PACK):

@@ -17,39 +17,50 @@ ALU = mybir.AluOpType
 
 P = 128
 PACK = 4
+GROUP = 16
+BLOCK = 8
+QUADRANT = 32
+LINE = 4
+
+D_WORD_CUTS = (0, 1024, 1536, 2048)
+
 CHUNKS = (((0, 128), (128, 192)), ((192, 256),))
 
 
-def tile_picked_hpqgaphaar_none_p_kernel(tc, x_words, x_scales, d_words, d_scales, gn, w1, offs, k1, n1, n2, n3, n4, out):
+def tile_picked_hpqgaphaar_none_p_kernel(
+    tc, x_words, x_scales, d_words, d_scales, gn, w1, offs, k1, n1, n2, n3, n4, out
+):
     nc = tc.nc
     with ExitStack() as ctx:
         lists = ctx.enter_context(tc.tile_pool(name="lists", bufs=1))
         sb = ctx.enter_context(tc.tile_pool(name="sb", bufs=1))
         psum = ctx.enter_context(tc.psum_pool(name="psum", bufs=1))
 
-        k1_t = lists.tile([P, H // 16], U16, name="k1_t")
-        offs_t = lists.tile([P, S // 16], U16, name="offs_t")
-        n1_t = lists.tile([P, S // 16], U16, name="n1_t")
-        n2_t = lists.tile([P, S // 16], U16, name="n2_t")
-        n3_t = lists.tile([P, W // 16], U16, name="n3_t")
-        n4_t = lists.tile([P, W // 16], U16, name="n4_t")
+        k1_t = lists.tile([P, H // GROUP], U16, name="k1_t")
+        offs_t = lists.tile([P, S // GROUP], U16, name="offs_t")
+        n1_t = lists.tile([P, S // GROUP], U16, name="n1_t")
+        n2_t = lists.tile([P, S // GROUP], U16, name="n2_t")
+        n3_t = lists.tile([P, W // GROUP], U16, name="n3_t")
+        n4_t = lists.tile([P, W // GROUP], U16, name="n4_t")
 
         ds_win = sb.tile([P, G], U8, name="ds_win", align_bytes=64)
         xs_win = sb.tile([P, T], U8, name="xs_win", align_bytes=64)
         gn_t = sb.tile([P, PACK], F32, name="gn_t")
         nc.vector.memset(xs_win[:].bitcast(I32), 0)
-        nc.sync.dma_start(xs_win[0:P:8, :].bitcast(I32), x_scales[0].bitcast(I32))
+        nc.sync.dma_start(xs_win[0:P:BLOCK, :].bitcast(I32), x_scales[0].bitcast(I32))
         nc.sync.dma_start(k1_t[:], k1)
-        nc.sync.dma_start(ds_win[:].bitcast(I32), d_scales[0].bitcast(I32).unsqueeze(1).broadcast_to([16, 8, G // 4]))
+        d_rows = d_scales[0].bitcast(I32).unsqueeze(1).broadcast_to([P // BLOCK, BLOCK, G // 4])
+        nc.sync.dma_start(ds_win[:].bitcast(I32), d_rows)
         nc.sync.dma_start(offs_t[:], offs)
+
         dw_win = sb.tile([P, G], I32, name="dw_win", tag="big_d", align_bytes=64)
         xw_win = sb.tile([P, T], I32, name="xw_win", align_bytes=64)
         d_src = d_words[0].rearrange("p n t -> p (n t)").bitcast(I32)
-        for lo, hi in ((0, 1024), (1024, 1280), (1280, 1536)):
+        for lo, hi in zip(D_WORD_CUTS[:-2], D_WORD_CUTS[1:-1]):
             nc.sync.dma_start(dw_win[:, lo:hi], d_src[:, lo:hi])
         nc.sync.dma_start(n1_t[:], n1)
         nc.sync.dma_start(n2_t[:], n2)
-        nc.sync.dma_start(dw_win[:, 1536:], d_src[:, 1536:])
+        nc.sync.dma_start(dw_win[:, D_WORD_CUTS[-2] :], d_src[:, D_WORD_CUTS[-2] :])
         nc.sync.dma_start(xw_win[:], x_words[0].rearrange("p n t -> p (n t)").bitcast(I32))
         nc.gpsimd.dma_start(gn_t[:], gn.rearrange("(p t) o -> p (t o)", t=PACK))
         nc.sync.dma_start(n3_t[:], n3)
@@ -69,8 +80,11 @@ def tile_picked_hpqgaphaar_none_p_kernel(tc, x_words, x_scales, d_words, d_scale
         )
         nc.vector.tensor_copy(sg[:, H:], xs_win[:].indirect(offs_t[:]))
         nc.vector.tensor_copy(dealt[:, H:].bitcast(I32), sg[:, H:].bitcast(I32))
-        for q in range(0, P, 32):
-            nc.scalar.dma_start(plane[q : q + 4, :].bitcast(I32), dealt[q : q + 32 : 8, :].bitcast(I32))
+        for q in range(0, P, QUADRANT):
+            nc.scalar.dma_start(
+                plane[q : q + QUADRANT // BLOCK, :].bitcast(I32),
+                dealt[q : q + QUADRANT : BLOCK, :].bitcast(I32),
+            )
 
         dg = sb.tile([P, H], U32, name="dg", tag="gathered", align_bytes=64)
         dq = sb.tile([P, H], U32, name="dq", align_bytes=64)
@@ -111,8 +125,8 @@ def tile_picked_hpqgaphaar_none_p_kernel(tc, x_words, x_scales, d_words, d_scale
             cols = slice(half * (N // 2), (half + 1) * (N // 2))
             wb = w_bf[:, cols.start * PACK : cols.stop * PACK]
             nc.vector.tensor_copy(
-                wb.rearrange("p (c i j) -> p c j i", i=4, j=PACK),
-                w_raw[:, :, cols].rearrange("p j (c i) -> p c j i", i=4),
+                wb.rearrange("p (c i j) -> p c j i", i=LINE, j=PACK),
+                w_raw[:, :, cols].rearrange("p j (c i) -> p c j i", i=LINE),
             )
             nc.vector.quantize_mx(out=wq[:, cols].bitcast(FP8X4), scales=ws[:, cols], in_=wb)
 
@@ -120,7 +134,7 @@ def tile_picked_hpqgaphaar_none_p_kernel(tc, x_words, x_scales, d_words, d_scale
         zs = sb.tile([P, S], U8, name="zs", align_bytes=64)
         h2w = [sb.tile([P, S], F32, name=f"h2w{m}") for m in range(PACK)]
 
-        def second(m, lo, hi, tag):
+        def second_product(m, lo, hi, tag):
             bank = psum.tile([P, hi - lo], F32, name=f"h2b{m}_{lo}", tag=tag)
             nc.tensor.matmul_mx(
                 out=bank[:],
@@ -139,18 +153,22 @@ def tile_picked_hpqgaphaar_none_p_kernel(tc, x_words, x_scales, d_words, d_scale
             picked = sb.tile([P, 2, PACK, hi - lo], F32, name=f"picked{c}", tag=f"picked{c}")
             g1, g2 = picked[:, 0], picked[:, 1]
             for t in range(PACK):
-                nc.scalar.activation(g1[:, t, :], hw[t][:].indirect(n1_t[:, lo // 16 : hi // 16]), COPY)
-                nc.scalar.activation(g2[:, t, :], hw[t][:].indirect(n2_t[:, lo // 16 : hi // 16]), COPY)
+                nc.scalar.activation(g1[:, t, :], hw[t][:].indirect(n1_t[:, lo // GROUP : hi // GROUP]), COPY)
+                nc.scalar.activation(g2[:, t, :], hw[t][:].indirect(n2_t[:, lo // GROUP : hi // GROUP]), COPY)
             zb = sb.tile([P, (hi - lo) * PACK], BF16, name=f"zb{c}", tag="rounded", align_bytes=64)
             nc.vector.tensor_tensor(
-                zb[:].rearrange("p (c i t) -> p c t i", i=4, t=PACK),
-                g1.rearrange("p t (c i) -> p c t i", i=4),
-                g2.rearrange("p t (c i) -> p c t i", i=4),
+                zb[:].rearrange("p (c i t) -> p c t i", i=LINE, t=PACK),
+                g1.rearrange("p t (c i) -> p c t i", i=LINE),
+                g2.rearrange("p t (c i) -> p c t i", i=LINE),
                 ALU.subtract,
             )
             for a, b in pieces:
-                nc.vector.quantize_mx(out=zq[:, a:b].bitcast(FP8X4), scales=zs[:, a:b], in_=zb[:, (a - lo) * PACK : (b - lo) * PACK])
-                first_banks.append((a, b, second(0, a, b, f"bank{4 + len(first_banks)}")))
+                nc.vector.quantize_mx(
+                    out=zq[:, a:b].bitcast(FP8X4),
+                    scales=zs[:, a:b],
+                    in_=zb[:, (a - lo) * PACK : (b - lo) * PACK],
+                )
+                first_banks.append((a, b, second_product(0, a, b, f"bank{PACK + len(first_banks)}")))
         for a, b, bank in first_banks:
             nc.scalar.copy(h2w[0][:, a:b], bank[:])
 
@@ -173,8 +191,8 @@ def tile_picked_hpqgaphaar_none_p_kernel(tc, x_words, x_scales, d_words, d_scale
 
         held = pair(0)
         for m in range(1, PACK):
-            nc.vector.tensor_copy(h2w[m][:], second(m, 0, S, f"bank{m}")[:])
-            nxt = pair(m)
+            nc.vector.tensor_copy(h2w[m][:], second_product(m, 0, S, f"bank{m}")[:])
+            ahead = pair(m)
             put(m - 1, *held)
-            held = nxt
+            held = ahead
         put(PACK - 1, *held)

from contextlib import ExitStack

import concourse.mybir as mybir

K, T, S, N, G, H, W = 512, 2048, 256, 512, 2048, 512, 128
FLOPS = 2 * K * H * S + 2 * H * N * S

F32 = mybir.dt.float32
BF16 = mybir.dt.bfloat16
I32 = mybir.dt.int32
U32 = mybir.dt.uint32
U16 = mybir.dt.uint16
U8 = mybir.dt.uint8
FP8X4 = mybir.dt.float8_e4m3fn_x4
COPY = mybir.ActivationFunctionType.Copy
ALU = mybir.AluOpType

P = 128
PACK = 4
GROUP = 16
BLOCK = 8
QUADRANT = 32
LINE = 4

D_WORD_CUTS = (0, 1024, 1536, 2048)

CHUNKS = (((0, 128), (128, 192)), ((192, 256),))


def tile_picked_hpqgaphaar_none_p_kernel(
    tc, x_words, x_scales, d_words, d_scales, gn, w1, offs, k1, n1, n2, n3, n4, out
):
    nc = tc.nc
    with ExitStack() as ctx:
        lists = ctx.enter_context(tc.tile_pool(name="lists", bufs=1))
        sb = ctx.enter_context(tc.tile_pool(name="sb", bufs=1))
        psum = ctx.enter_context(tc.psum_pool(name="psum", bufs=1))

        k1_t = lists.tile([P, H // GROUP], U16, name="k1_t")
        offs_t = lists.tile([P, S // GROUP], U16, name="offs_t")
        n1_t = lists.tile([P, S // GROUP], U16, name="n1_t")
        n2_t = lists.tile([P, S // GROUP], U16, name="n2_t")
        n3_t = lists.tile([P, W // GROUP], U16, name="n3_t")
        n4_t = lists.tile([P, W // GROUP], U16, name="n4_t")

        ds_win = sb.tile([P, G], U8, name="ds_win", align_bytes=64)
        xs_win = sb.tile([P, T], U8, name="xs_win", align_bytes=64)
        gn_t = sb.tile([P, PACK], F32, name="gn_t")
        nc.vector.memset(xs_win[:].bitcast(I32), 0)
        nc.sync.dma_start(xs_win[0:P:BLOCK, :].bitcast(I32), x_scales[0].bitcast(I32))
        nc.sync.dma_start(k1_t[:], k1)
        d_rows = d_scales[0].bitcast(I32).unsqueeze(1).broadcast_to([P // BLOCK, BLOCK, G // 4])
        nc.sync.dma_start(ds_win[:].bitcast(I32), d_rows)
        nc.sync.dma_start(offs_t[:], offs)

        dw_win = sb.tile([P, G], I32, name="dw_win", tag="big_d", align_bytes=64)
        xw_win = sb.tile([P, T], I32, name="xw_win", align_bytes=64)
        d_src = d_words[0].rearrange("p n t -> p (n t)").bitcast(I32)
        for lo, hi in zip(D_WORD_CUTS[:-2], D_WORD_CUTS[1:-1]):
            nc.sync.dma_start(dw_win[:, lo:hi], d_src[:, lo:hi])
        nc.sync.dma_start(n1_t[:], n1)
        nc.sync.dma_start(n2_t[:], n2)
        nc.sync.dma_start(dw_win[:, D_WORD_CUTS[-2] :], d_src[:, D_WORD_CUTS[-2] :])
        nc.sync.dma_start(xw_win[:], x_words[0].rearrange("p n t -> p (n t)").bitcast(I32))
        nc.gpsimd.dma_start(gn_t[:], gn.rearrange("(p t) o -> p (t o)", t=PACK))
        nc.sync.dma_start(n3_t[:], n3)
        nc.sync.dma_start(n4_t[:], n4)

        gs = sb.tile([P, PACK], F32, name="gs", tag="picked1")
        nc.scalar.activation(gs[:], gn_t[:], COPY, scale=0.0625)

        sg = sb.tile([P, H + S], U8, name="sg", tag="gathered", align_bytes=64)
        plane = sb.tile([P, H + S], U8, name="plane", align_bytes=64)
        dealt = sb.tile([P, H + S], U8, name="dealt", align_bytes=64)
        nc.vector.memset(plane[:].bitcast(I32), 0)
        nc.vector.tensor_copy(sg[:, :H], ds_win[:].indirect(k1_t[:]))
        nc.vector.tensor_copy(
            dealt[:, :H].rearrange("p (t m) -> p t m", t=PACK),
            sg[:, :H].rearrange("p (m t) -> p t m", t=PACK),
        )
        nc.vector.tensor_copy(sg[:, H:], xs_win[:].indirect(offs_t[:]))
        nc.vector.tensor_copy(dealt[:, H:].bitcast(I32), sg[:, H:].bitcast(I32))
        for q in range(0, P, QUADRANT):
            nc.scalar.dma_start(
                plane[q : q + QUADRANT // BLOCK, :].bitcast(I32),
                dealt[q : q + QUADRANT : BLOCK, :].bitcast(I32),
            )

        dg = sb.tile([P, H], U32, name="dg", tag="gathered", align_bytes=64)
        dq = sb.tile([P, H], U32, name="dq", align_bytes=64)
        xq = sb.tile([P, S], U32, name="xq", align_bytes=64)
        nc.vector.tensor_copy(dg[:], dw_win[:].bitcast(U32).indirect(k1_t[:]))
        nc.vector.tensor_copy(
            dq[:].bitcast(I32).rearrange("p (t m) -> p t m", t=PACK),
            dg[:].bitcast(I32).rearrange("p (m t) -> p t m", t=PACK),
        )
        nc.vector.tensor_copy(xq[:], xw_win[:].bitcast(U32).indirect(offs_t[:]))

        w_raw = sb.tile([P, PACK, N], F32, name="w_raw", tag="big_d", align_bytes=64)
        nc.sync.dma_start(w_raw[:], w1.rearrange("(p j) m -> p j m", j=PACK))

        hw = []
        for t in range(PACK):
            bank = psum.tile([P, S], F32, name=f"hb{t}", tag=f"bank{t}")
            nc.tensor.matmul_mx(
                out=bank[:],
                lhsT=dq[:, t * P : (t + 1) * P].bitcast(FP8X4),
                lhsT_scale=plane[:, t * P : (t + 1) * P],
                rhs=xq[:].bitcast(FP8X4),
                rhs_scale=plane[:, H:],
                start=True,
                stop=True,
            )
            win = sb.tile([P, S], F32, name=f"hw{t}")
            if t == 0:
                nc.scalar.activation(win[:], bank[:], COPY, scale=gs[:, t : t + 1])
            else:
                nc.vector.tensor_scalar(win[:], bank[:], gs[:, t : t + 1], None, ALU.mult)
            hw.append(win)

        wq = sb.tile([P, N], U32, name="wq", align_bytes=64)
        ws = sb.tile([P, N], U8, name="ws", align_bytes=64)
        w_bf = sb.tile([P, N * PACK], BF16, name="w_bf", tag="rounded", align_bytes=64)
        for half in range(2):
            cols = slice(half * (N // 2), (half + 1) * (N // 2))
            wb = w_bf[:, cols.start * PACK : cols.stop * PACK]
            nc.vector.tensor_copy(
                wb.rearrange("p (c i j) -> p c j i", i=LINE, j=PACK),
                w_raw[:, :, cols].rearrange("p j (c i) -> p c j i", i=LINE),
            )
            nc.vector.quantize_mx(out=wq[:, cols].bitcast(FP8X4), scales=ws[:, cols], in_=wb)

        zq = sb.tile([P, S], U32, name="zq", align_bytes=64)
        zs = sb.tile([P, S], U8, name="zs", align_bytes=64)
        h2w = [sb.tile([P, S], F32, name=f"h2w{m}") for m in range(PACK)]

        def second_product(m, lo, hi, tag):
            bank = psum.tile([P, hi - lo], F32, name=f"h2b{m}_{lo}", tag=tag)
            nc.tensor.matmul_mx(
                out=bank[:],
                lhsT=wq[:, m * P : (m + 1) * P].bitcast(FP8X4),
                lhsT_scale=ws[:, m * P : (m + 1) * P],
                rhs=zq[:, lo:hi].bitcast(FP8X4),
                rhs_scale=zs[:, lo:hi],
                start=True,
                stop=True,
            )
            return bank

        first_banks = []
        for c, pieces in enumerate(CHUNKS):
            lo, hi = pieces[0][0], pieces[-1][1]
            picked = sb.tile([P, 2, PACK, hi - lo], F32, name=f"picked{c}", tag=f"picked{c}")
            g1, g2 = picked[:, 0], picked[:, 1]
            for t in range(PACK):
                nc.scalar.activation(g1[:, t, :], hw[t][:].indirect(n1_t[:, lo // GROUP : hi // GROUP]), COPY)
                nc.scalar.activation(g2[:, t, :], hw[t][:].indirect(n2_t[:, lo // GROUP : hi // GROUP]), COPY)
            zb = sb.tile([P, (hi - lo) * PACK], BF16, name=f"zb{c}", tag="rounded", align_bytes=64)
            nc.vector.tensor_tensor(
                zb[:].rearrange("p (c i t) -> p c t i", i=LINE, t=PACK),
                g1.rearrange("p t (c i) -> p c t i", i=LINE),
                g2.rearrange("p t (c i) -> p c t i", i=LINE),
                ALU.subtract,
            )
            for a, b in pieces:
                nc.vector.quantize_mx(
                    out=zq[:, a:b].bitcast(FP8X4),
                    scales=zs[:, a:b],
                    in_=zb[:, (a - lo) * PACK : (b - lo) * PACK],
                )
                first_banks.append((a, b, second_product(0, a, b, f"bank{PACK + len(first_banks)}")))
        for a, b, bank in first_banks:
            nc.scalar.copy(h2w[0][:, a:b], bank[:])

        def pair(m):
            pa = sb.tile([P, W], F32, name=f"pa{m}")
            pb = sb.tile([P, W], F32, name=f"pb{m}")
            nc.scalar.activation(pa[:], h2w[m][:].indirect(n3_t[:]), COPY)
            nc.scalar.activation(pb[:], h2w[m][:].indirect(n4_t[:]), COPY)
            sm = sb.tile([P, W], F32, name=f"sm{m}")
            df = sb.tile([P, W], F32, name=f"df{m}")
            nc.vector.tensor_tensor(sm[:], pa[:], pb[:], ALU.add)
            nc.vector.tensor_tensor(df[:], pa[:], pb[:], ALU.subtract)
            return sm, df

        def put(m, sm, df):
            res = sb.tile([P, S], F32, name=f"res{m}")
            nc.scalar.activation(res[:].indirect(n3_t[:]), sm[:], COPY, scale=0.75)
            nc.scalar.activation(res[:].indirect(n4_t[:]), df[:], COPY)
            nc.sync.dma_start(out[m * P : (m + 1) * P, :], res[:])

        held = pair(0)
        for m in range(1, PACK):
            nc.vector.tensor_copy(h2w[m][:], second_product(m, 0, S, f"bank{m}")[:])
            ahead = pair(m)
            put(m - 1, *held)
            held = ahead
        put(PACK - 1, *held)
